import numpy as np
import ml_dtypes


def mxq(x, axis, fmt="e4m3"):
    dtype, down = {"e4m3": (ml_dtypes.float8_e4m3fn, 7), "e5m2": (ml_dtypes.float8_e5m2, 14)}[fmt]
    v = np.moveaxis(np.asarray(x, np.float32).astype(ml_dtypes.bfloat16).astype(np.float64), axis, -1)
    blocks = v.reshape(v.shape[:-1] + (-1, 32))
    amax = np.abs(blocks).max(-1, keepdims=True)
    byte = np.maximum(np.where(amax > 0, np.frexp(amax)[1] - 1 + 127, 0) - down, 1)
    scale = np.exp2(byte - 127.0)
    codes = (blocks / scale).astype(np.float32).astype(dtype).astype(np.float64)
    return np.moveaxis((codes * scale).reshape(v.shape), -1, axis)


WIDE = False


def mx_kscale(k):
    if not WIDE:
        return np.ones(k)
    levels = np.array([10, -10, 5, -5, 0])
    if k % 512:
        return np.exp2(np.random.permutation(np.resize(levels, k // 32))).repeat(32)
    a = np.empty((k // 512, 16))
    for p in range(k // 512):
        a[p, :8] = np.random.permutation(np.resize(levels, 8))
        for g in range(8):
            far = levels[np.abs(levels - a[p, g]) >= 10]
            a[p, g + 8] = far[np.random.randint(len(far))]
    return np.exp2(a.ravel()).repeat(32)


def f64(x):
    return np.asarray(x).astype(np.float64)


def striped(idx):
    return np.tile(idx.reshape(-1, 16).T, (8, 1)).astype(np.uint16)


def unstriped(offs):
    return offs[:16].T.reshape(-1).astype(np.int64)


E2M1 = np.array([0.0, 0.5, 1.0, 1.5, 2.0, 3.0, 4.0, 6.0, -0.0, -0.5, -1.0, -1.5, -2.0, -3.0, -4.0, -6.0])


def pack_weight(w, fmt):
    k, n = w.shape
    w = f64(np.asarray(w, np.float32).astype(ml_dtypes.bfloat16)).reshape(k // 32, 32, n)
    amax = np.abs(w).max(1)
    if fmt == "e4m3":
        byte = np.frexp(amax)[1] - 1 + 127 - 7
    else:
        mant, ex = np.frexp(amax / 6.0)
        byte = np.where(mant > 0.5, ex, ex - 1) + 127
    byte = np.clip(np.where(amax > 0, byte, 1), 1, 254)
    scaled = (w * np.exp2(127.0 - byte)[:, None, :]).reshape(k, n).astype(np.float32)
    by_word = np.ascontiguousarray(scaled.reshape(k // 512, 128, 4, n).transpose(0, 1, 3, 2))
    if fmt == "e4m3":
        words = by_word.astype(ml_dtypes.float8_e4m3fn).view(np.uint8)
    else:
        c = by_word.astype(ml_dtypes.float4_e2m1fn).view(np.uint8) & 0xF
        words = (c[..., 0::2] | (c[..., 1::2] << 4)).reshape(k // 512, 128, 2 * n)
    return np.ascontiguousarray(words), np.ascontiguousarray(byte.astype(np.uint8).reshape(k // 512, 16, n))


def unpack_weight(words, scales, fmt):
    g, _, n = scales.shape
    words = np.ascontiguousarray(words).reshape(g, 128, n, -1)
    if fmt == "e4m3":
        vals = words.view(ml_dtypes.float8_e4m3fn).astype(np.float64)
    else:
        nib = np.empty((g, 128, n, 4), np.uint8)
        nib[..., 0::2] = words & 0xF
        nib[..., 1::2] = words >> 4
        vals = E2M1[nib]
    vals = vals * np.repeat(np.exp2(scales.astype(np.float64) - 127.0), 8, axis=1)[..., None]
    return vals.transpose(0, 1, 3, 2).reshape(g * 512, n)


def planes(y):
    n, m = y.shape
    v = y.astype(np.float32).astype(ml_dtypes.bfloat16).astype(np.float64).reshape(n // 32, 32, m)
    top = np.abs(v).max(1)
    byte = np.clip(np.where(top > 0, np.frexp(top)[1] - 1 + 127 - 7, 1), 1, 254)
    codes = (v * np.exp2(127.0 - byte)[:, None, :]).reshape(n, m).astype(np.float32).astype(ml_dtypes.float8_e4m3fn).view(np.uint8)
    words = codes.reshape(n // 512, 128, 4, m).transpose(0, 1, 3, 2)
    return np.ascontiguousarray(words), np.ascontiguousarray(byte.astype(np.uint8).reshape(n // 512, 16, m))


def relu(v):
    return np.maximum(v, 0.0)


K, T, E, C, H, N, TOP = 1024, 512, 16, 128, 512, 512, 4


def by_expert(wq, xq):
    return np.concatenate([wq[e].T @ xq[:, e * C:(e + 1) * C] for e in range(E)], axis=1)


def setup_inputs():
    n = np.random.standard_normal
    s = mx_kscale(K)
    u = mx_kscale(H)
    deal = np.repeat(np.arange(E), C).reshape(TOP, T)[:, np.random.permutation(T)]
    deal = np.take_along_axis(deal, np.argsort(np.random.rand(TOP, T), axis=0), axis=0)
    for _ in range(8):
        s_, t_ = np.random.permutation(T).reshape(2, -1); r = np.random.randint(TOP, size=T // 2); x, y = deal[r, s_].copy(), deal[r, t_].copy()
        ok = ~((deal[:, s_] == y).any(0) | (deal[:, t_] == x).any(0)); deal[r[ok], s_[ok]] = y[ok]; deal[r[ok], t_[ok]] = x[ok]
    order = np.lexsort((np.random.rand(TOP * T), deal.reshape(-1)))
    slot_token = order % T; pos = np.empty(TOP * T, np.int64); pos[order] = np.arange(TOP * T); pos = pos.reshape(TOP, T)
    g = np.random.uniform(0.5, 1.5, (TOP, T)); g = g / g.sum(0)
    x = pack_weight(n((K, T)) * s[:, None], "e4m3")
    w1 = [pack_weight(m, "e2m1") for m in n((E, K, H)) / np.sqrt(K) / s[None, :, None] * u]
    return {
        "x_words": x[0],
        "x_scales": x[1],
        "w1_words": np.stack([m[0] for m in w1]),
        "w1_scales": np.stack([m[1] for m in w1]),
        "w2": (n((H, N)) / np.sqrt(H) / u[:, None]).astype(np.float32),
        "gate": np.stack([np.tile(r, (128, 1)) for r in g]).astype(np.float32),
        "offs": striped(slot_token),
        "pos1": striped(pos[0]),
        "pos2": striped(pos[1]),
        "pos3": striped(pos[2]),
        "pos4": striped(pos[3]),
    }


def reference(x_words, x_scales, w1_words, w1_scales, w2, gate, offs, pos1, pos2, pos3, pos4):
    w1 = np.stack([unpack_weight(w1_words[e], w1_scales[e], "e2m1") for e in range(E)])
    w2q = mxq(f64(w2), 0, "e4m3")
    idx = unstriped(offs)
    xq = unpack_weight(x_words, x_scales, "e4m3")[:, idx]
    h = relu(by_expert(w1, xq))
    c = sum(f64(gate[r, :1]) * h[:, unstriped(p)] for r, p in enumerate((pos1, pos2, pos3, pos4)))
    out_0 = w2q.T @ mxq(c, 0, "e4m3")
    return (out_0,) + planes(out_0)

from contextlib import ExitStack

import concourse.mybir as mybir
from concourse.masks import make_identity

K, T, E, C, H, N, TOP = 1024, 512, 16, 128, 512, 512, 4
FLOPS = 2 * K * H * E * C + 2 * H * N * T

F32 = mybir.dt.float32
BF16 = mybir.dt.bfloat16
I32 = mybir.dt.int32
U32 = mybir.dt.uint32
U16 = mybir.dt.uint16
U8 = mybir.dt.uint8
FP8X4 = mybir.dt.float8_e4m3fn_x4
FP4X4 = mybir.dt.float4_e2m1fn_x4
MULT = mybir.AluOpType.mult
ADD = mybir.AluOpType.add
COPY = mybir.ActivationFunctionType.Copy
RELU = mybir.ActivationFunctionType.Relu

P = 128
PASSES = K // 512
SLOTS = E * C
GROUP = 4
GROUPS = E // GROUP
GROUP_SLOTS = GROUP * C
BLOCKS = H // P
CHUNK = 256
SUBS = CHUNK // P
SPARE = 256
ON_VECTOR = ("VVVV", "VSSS", "SSSV", "SSSV", "SSSS", "SSSS", "SSSV", "SSSV")


def tile_moe_sdn_lin_relu_kernel(
    tc, x_words, x_scales, w1_words, w1_scales, w2, gate, offs, pos1, pos2, pos3, pos4, out_0, out_1, out_2
):
    nc = tc.nc
    with ExitStack() as ctx:
        lists = ctx.enter_context(tc.tile_pool(name="lists", bufs=1))
        held = ctx.enter_context(tc.tile_pool(name="held", bufs=1))
        ring = ctx.enter_context(tc.tile_pool(name="ring", bufs=2))
        picks = ctx.enter_context(tc.tile_pool(name="picks", bufs=8))
        psum = ctx.enter_context(tc.psum_pool(name="psum", bufs=6))
        psum2 = ctx.enter_context(tc.psum_pool(name="psum2", bufs=2))

        offs_sb = lists.tile([P, SLOTS // 16], U16, name="offs_sb")
        pos_sb = [lists.tile([P, T // 16], U16, name=f"pos_sb{r}") for r in range(TOP)]

        token_scales = held.tile([P, PASSES * T + SPARE], U8, name="token_scales", align_bytes=64)
        token_words = held.tile([P, PASSES * T + SPARE], I32, name="token_words", align_bytes=64)
        w1_codes = [held.tile([P, GROUP * PASSES * 2 * H], U8, name=f"w1_codes{g}", align_bytes=64) for g in range(GROUPS)]
        w1_planes = [held.tile([P, GROUP * PASSES * H], U8, name=f"w1_planes{g}", align_bytes=64) for g in range(GROUPS)]
        gate_rows = held.tile([P, P], F32, name="gate_rows")
        gate_cols = held.tile([P, TOP * T // P], F32, name="gate_cols")
        identity = held.tile([P, P], F32, name="identity")
        hidden = [held.tile([P, SLOTS], F32, name=f"hidden{d}") for d in range(BLOCKS)]

        nc.gpsimd.memset(token_scales[:].bitcast(I32), 0)
        nc.sync.dma_start(offs_sb[:], offs)
        scale_rows = x_scales.rearrange("s (q r) t -> r q s t", r=4)
        for r in range(4):
            nc.sync.dma_start(
                out=token_scales[r:P:32, 0 : PASSES * T].bitcast(I32).rearrange("q (s t) -> q s t", s=PASSES),
                in_=scale_rows[r].bitcast(I32),
            )
        nc.sync.dma_start(
            out=token_words[:, 0 : PASSES * T].rearrange("p (s t) -> p s t", s=PASSES),
            in_=x_words.rearrange("s p t d -> p s (t d)").bitcast(I32),
        )
        nc.vector.memset(token_words[:, PASSES * T :], 0)
        for g in range(GROUPS):
            engine = nc.vector if g < 2 else nc.gpsimd
            engine.memset(w1_planes[g][:].bitcast(I32), 0)
        nc.gpsimd.memset(gate_rows[:], 0.0)
        make_identity(nc, identity[:])

        def load_codes(g, first, last):
            rows = slice(first * PASSES, last * PASSES)
            nc.sync.dma_start(
                out=w1_codes[g][:].bitcast(I32).rearrange("p (m c) -> p m c", m=GROUP * PASSES)[:, rows, :],
                in_=w1_words[g * GROUP + first : g * GROUP + last].rearrange("e s p c -> p (e s) c").bitcast(I32),
            )

        def load_planes(g):
            rows = w1_scales[g * GROUP : (g + 1) * GROUP].rearrange("e s (q r) n -> r q (e s) n", r=4)
            for r in range(4):
                nc.sync.dma_start(
                    out=w1_planes[g][r:P:32, :].bitcast(I32).rearrange("q (m n) -> q m n", m=GROUP * PASSES),
                    in_=rows[r].bitcast(I32),
                )

        w2_raw = held.tile([P, 4, N], F32, name="w2_raw")
        for g in range(GROUPS - 1):
            load_codes(g, 0, GROUP)
            load_planes(g)
            if g == 1:
                nc.sync.dma_start(
                    out=gate_rows[0 : TOP * T // P, :], in_=gate[:, 0, :].rearrange("r (c t) -> r c t", t=P)
                )
                for r, pos in enumerate((pos1, pos2, pos3, pos4)):
                    nc.sync.dma_start(pos_sb[r][:], pos)
                nc.sync.dma_start(out=w2_raw[:], in_=w2.rearrange("(p j) n -> p j n", j=4))
        load_planes(GROUPS - 1)
        load_codes(GROUPS - 1, 0, GROUP // 2)
        load_codes(GROUPS - 1, GROUP // 2, GROUP)

        for g in range(GROUPS):
            slots = slice(g * GROUP_SLOTS, (g + 1) * GROUP_SLOTS)
            entries = offs_sb[:, g * GROUP_SLOTS // 16 : (g + 1) * GROUP_SLOTS // 16]
            slot_scales = [
                held.tile([P, GROUP_SLOTS], U8, name=f"slot_scales{g}_{s}", align_bytes=64) for s in range(PASSES)
            ]
            for s in range(PASSES):
                nc.vector.tensor_copy(slot_scales[s][:], token_scales[:, s * T : (s + 1) * T + SPARE].indirect(entries))
            slot_words = [
                held.tile([P, GROUP_SLOTS], U32, name=f"slot_words{g}_{s}", align_bytes=64) for s in range(PASSES)
            ]
            parts = 2 if g == GROUPS - 1 else 1
            size = GROUP // parts
            banks = {}
            for part in range(parts):
                first = part * size
                for s in range(PASSES):
                    window = token_words[:, s * T : (s + 1) * T + SPARE].bitcast(U32)
                    nc.vector.tensor_copy(
                        slot_words[s][:, first * C : (first + size) * C],
                        window.indirect(entries[:, first * C // 16 : (first + size) * C // 16]),
                    )
                for d in range(BLOCKS):
                    if part == 0:
                        banks[d] = psum.tile([P, 512], F32, name="bank")
                    for u in range(first, first + size):
                        own = slice(u * C, (u + 1) * C)
                        for s in range(PASSES):
                            m = u * PASSES + s
                            nc.tensor.matmul_mx(
                                out=banks[d][:, own],
                                lhsT=w1_codes[g][:, 2 * (m * H + d * P) : 2 * (m * H + (d + 1) * P)].bitcast(FP4X4),
                                lhsT_scale=w1_planes[g][:, m * H + d * P : m * H + (d + 1) * P],
                                rhs=slot_words[s][:, own].bitcast(FP8X4),
                                rhs_scale=slot_scales[s][:, own],
                                start=(s == 0),
                                stop=(s == PASSES - 1),
                            )
                    if part == parts - 1:
                        nc.scalar.activation(out=hidden[d][:, slots], in_=banks[d][:], func=RELU)
            if g == 2:
                bank = psum2.tile([P, 512], F32, name="back")
                nc.tensor.transpose(bank[:, 0:P], gate_rows[:], identity[:])
                nc.scalar.copy(out=gate_cols[:], in_=bank[:, 0 : TOP * T // P])
                w2_grouped = held.tile([P, N * 4], BF16, name="w2_grouped", align_bytes=64)
                nc.scalar.copy(
                    out=w2_grouped[:].rearrange("p (d m j) -> p m d j", d=4, j=4),
                    in_=w2_raw[:].rearrange("p j (m d) -> p m d j", d=4),
                )

        w2_codes = held.tile([P, N], U32, name="w2_codes", align_bytes=64)
        w2_plane = held.tile([P, N], U8, name="w2_plane", align_bytes=64)
        nc.vector.quantize_mx(out=w2_codes[:].bitcast(FP8X4), scales=w2_plane[:], in_=w2_grouped[:])

        y_codes = held.tile([P, T], U32, name="y_codes", align_bytes=64)
        y_plane = held.tile([P, T], U8, name="y_plane", align_bytes=64)
        y_rows = out_0.rearrange("(p d) t -> p d t", d=4)
        y_words = out_1[0].rearrange("p t d -> p (t d)").bitcast(I32)

        def fetch(chunk, r):
            banks = [psum.tile([P, 512], F32, name="bank") for sub in range(SUBS)]
            for d in range(BLOCKS):
                picked = picks.tile([P, CHUNK], F32, name="picked")
                source = hidden[d][:].indirect(pos_sb[r][:, chunk * CHUNK // 16 : (chunk + 1) * CHUNK // 16])
                if ON_VECTOR[chunk * TOP + r][d] == "V":
                    nc.vector.tensor_copy(picked[:], source)
                else:
                    nc.scalar.activation(out=picked[:], in_=source, func=COPY)
                for sub in range(SUBS):
                    nc.tensor.transpose(
                        banks[sub][:, d * P : (d + 1) * P], picked[:, sub * P : (sub + 1) * P], identity[:]
                    )
            return banks

        def weigh(chunk, r, banks, sums):
            for sub in range(SUBS):
                column = r * (T // P) + chunk * SUBS + sub
                weight = gate_cols[:, column : column + 1]
                total = ring.tile([P, H], BF16 if r == TOP - 1 else F32, name=f"sum{r}")
                if r == 0:
                    nc.vector.tensor_scalar(out=total[:], in0=banks[sub][:], scalar1=weight, scalar2=None, op0=MULT)
                else:
                    nc.vector.scalar_tensor_tensor(
                        out=total[:], in0=banks[sub][:], scalar=weight, in1=sums[sub][:], op0=MULT, op1=ADD
                    )
                sums[sub] = total

        def finish(chunk, sums):
            last = chunk == T // CHUNK - 1
            empty = nc.scalar.copy if last else nc.vector.tensor_copy
            quantised = []
            for sub in range(SUBS):
                pairs = sums[sub][:].bitcast(F32)
                bank = psum2.tile([P, 512], F32, name="back")
                for u in range(2):
                    nc.tensor.transpose(bank[:, u * P : (u + 1) * P], pairs[:, u : 2 * P : 2], identity[:])
                c_grouped = ring.tile([P, 4 * P], BF16, name="c_grouped", align_bytes=64)
                empty(
                    out=c_grouped[:].bitcast(F32).rearrange("p (t u) -> p t u", u=2),
                    in_=bank[:, 0 : 2 * P].rearrange("p (u t) -> p t u", u=2),
                )
                quantised.append(c_grouped)
            for sub in range(SUBS):
                c_codes = ring.tile([P, P], U32, name="c_codes", align_bytes=64)
                c_plane = ring.tile([P, P], U8, name="c_plane", align_bytes=64)
                nc.vector.quantize_mx(out=c_codes[:].bitcast(FP8X4), scales=c_plane[:], in_=quantised[sub][:])
                quantised[sub] = (c_codes, c_plane)
            results = []
            for sub in range(SUBS):
                c_codes, c_plane = quantised[sub]
                bank = psum2.tile([P, 512], F32, name="back")
                for d in range(4):
                    columns = slice(d * P, (d + 1) * P)
                    nc.tensor.matmul_mx(
                        out=bank[:, columns],
                        lhsT=w2_codes[:, columns].bitcast(FP8X4),
                        lhsT_scale=w2_plane[:, columns],
                        rhs=c_codes[:].bitcast(FP8X4),
                        rhs_scale=c_plane[:],
                        start=True,
                        stop=True,
                    )
                y = ring.tile([P, 4, P], F32, name="y")
                nc.scalar.copy(out=y[:].rearrange("p d t -> p (d t)"), in_=bank[:])
                results.append(y)
            grouped = []
            for sub in range(SUBS):
                tokens = slice(chunk * CHUNK + sub * P, chunk * CHUNK + (sub + 1) * P)
                y = results[sub]
                nc.sync.dma_start(out=y_rows[:, :, tokens], in_=y[:])
                y_grouped = ring.tile([P, 4 * P], BF16, name="y_grouped", align_bytes=64)
                nc.vector.tensor_copy(
                    out=y_grouped[:].rearrange("p (c i d) -> p c d i", i=4, d=4),
                    in_=y[:].rearrange("p d (c i) -> p c d i", i=4),
                )
                grouped.append(y_grouped)
            for sub in range(SUBS):
                tokens = slice(chunk * CHUNK + sub * P, chunk * CHUNK + (sub + 1) * P)
                nc.vector.quantize_mx(
                    out=y_codes[:, tokens].bitcast(FP8X4), scales=y_plane[:, tokens], in_=grouped[sub][:]
                )
                nc.sync.dma_start(out=y_words[:, tokens], in_=y_codes[:, tokens].bitcast(I32))

        sums = [{} for chunk in range(T // CHUNK)]
        steps = [(chunk, r) for chunk in range(T // CHUNK) for r in range(TOP)]
        fetched = fetch(*steps[0])
        for index, (chunk, r) in enumerate(steps):
            ahead = fetch(*steps[index + 1]) if index + 1 < len(steps) else None
            weigh(chunk, r, fetched, sums[chunk])
            if r == TOP - 1:
                finish(chunk, sums[chunk])
            fetched = ahead
        for q in range(4):
            engine = nc.scalar if q % 2 else nc.sync
            engine.dma_start(
                out=out_2[0, 4 * q : 4 * q + 4, :].bitcast(I32), in_=y_plane[32 * q : 32 * q + 4, :].bitcast(I32)
            )
